import numpy as np
import ml_dtypes


def mxq(x, axis, fmt="e4m3"):
    dtype, down = {"e4m3": (ml_dtypes.float8_e4m3fn, 7), "e5m2": (ml_dtypes.float8_e5m2, 14)}[fmt]
    v = np.moveaxis(np.asarray(x, np.float32).astype(ml_dtypes.bfloat16).astype(np.float64), axis, -1)
    blocks = v.reshape(v.shape[:-1] + (-1, 32))
    amax = np.abs(blocks).max(-1, keepdims=True)
    byte = np.maximum(np.where(amax > 0, np.frexp(amax)[1] - 1 + 127, 0) - down, 1)
    scale = np.exp2(byte - 127.0)
    codes = (blocks / scale).astype(np.float32).astype(dtype).astype(np.float64)
    return np.moveaxis((codes * scale).reshape(v.shape), -1, axis)


WIDE = False


def mx_kscale(k):
    if not WIDE:
        return np.ones(k)
    levels = np.array([10, -10, 5, -5, 0])
    if k % 512:
        return np.exp2(np.random.permutation(np.resize(levels, k // 32))).repeat(32)
    a = np.empty((k // 512, 16))
    for p in range(k // 512):
        a[p, :8] = np.random.permutation(np.resize(levels, 8))
        for g in range(8):
            far = levels[np.abs(levels - a[p, g]) >= 10]
            a[p, g + 8] = far[np.random.randint(len(far))]
    return np.exp2(a.ravel()).repeat(32)


def f64(x):
    return np.asarray(x).astype(np.float64)


def striped(idx):
    return np.tile(np.asarray(idx).reshape(-1, 16).T, (8, 1)).astype(np.uint16)


def unstriped(offs):
    return offs[:16].T.reshape(-1).astype(np.int64)


E2M1 = np.array([0.0, 0.5, 1.0, 1.5, 2.0, 3.0, 4.0, 6.0, -0.0, -0.5, -1.0, -1.5, -2.0, -3.0, -4.0, -6.0])


def pack_weight(w, fmt):
    k, n = w.shape
    w = f64(np.asarray(w, np.float32).astype(ml_dtypes.bfloat16)).reshape(k // 32, 32, n)
    amax = np.abs(w).max(1)
    if fmt == "e4m3":
        byte = np.frexp(amax)[1] - 1 + 127 - 7
    else:
        mant, ex = np.frexp(amax / 6.0)
        byte = np.where(mant > 0.5, ex, ex - 1) + 127
    byte = np.clip(np.where(amax > 0, byte, 1), 1, 254)
    scaled = (w * np.exp2(127.0 - byte)[:, None, :]).reshape(k, n).astype(np.float32)
    by_word = np.ascontiguousarray(scaled.reshape(k // 512, 128, 4, n).transpose(0, 1, 3, 2))
    if fmt == "e4m3":
        words = by_word.astype(ml_dtypes.float8_e4m3fn).view(np.uint8)
    else:
        c = by_word.astype(ml_dtypes.float4_e2m1fn).view(np.uint8) & 0xF
        words = (c[..., 0::2] | (c[..., 1::2] << 4)).reshape(k // 512, 128, 2 * n)
    return np.ascontiguousarray(words), np.ascontiguousarray(byte.astype(np.uint8).reshape(k // 512, 16, n))


def unpack_weight(words, scales, fmt):
    g, _, n = scales.shape
    words = np.ascontiguousarray(words).reshape(g, 128, n, -1)
    if fmt == "e4m3":
        vals = words.view(ml_dtypes.float8_e4m3fn).astype(np.float64)
    else:
        nib = np.empty((g, 128, n, 4), np.uint8)
        nib[..., 0::2] = words & 0xF
        nib[..., 1::2] = words >> 4
        vals = E2M1[nib]
    vals = vals * np.repeat(np.exp2(scales.astype(np.float64) - 127.0), 8, axis=1)[..., None]
    return vals.transpose(0, 1, 3, 2).reshape(g * 512, n)


D, T, I, Q, E, U, J = 512, 2048, 512, 128, 512, 1024, 512


def setup_inputs():
    n = np.random.standard_normal
    idx = np.random.permutation(T)[:I]
    idx2 = np.random.permutation(U)[:J]
    fd = mx_kscale(D)
    fi = mx_kscale(I)
    fj = mx_kscale(J)
    ti = np.ones(T)
    ti[idx] = fi
    tj = np.ones(U)
    tj[idx2] = fj
    keysp = pack_weight(n((D, T)) / fd[:, None], "e4m3")
    return {
        "query": (n((D, Q)) * 0.45 / np.sqrt(D) * fd[:, None]).astype(np.float32),
        "keys_words": keysp[0],
        "keys_scales": keysp[1],
        "size": (np.random.uniform(0.5, 2.0, (1, I)) * fi).astype(np.float32),
        "vals": (n((E, T)) / ti).astype(np.float32),
        "equery": (n((D, Q)) * 1.0 / np.sqrt(D) * fd[:, None]).astype(np.float32),
        "ekeys": (n((D, U)) / fd[:, None]).astype(np.float32),
        "evals": (n((E, U)) / tj).astype(np.float32),
        "th": (np.random.uniform(0.0, 0.6, (Q, 1))).astype(np.float32),
        "ew": (np.random.uniform(0.002, 0.008, (1, J)) * fj).astype(np.float32),
        "offs": striped(idx),
        "offs2": striped(idx2),
    }


def reference(query, keys_words, keys_scales, size, vals, equery, ekeys, evals, th, ew, offs, offs2):
    idx = unstriped(offs)
    idx2 = unstriped(offs2)
    keysu = unpack_weight(keys_words, keys_scales, "e4m3")
    queryq = mxq(f64(query), 0, "e4m3")
    keysidxg = keysu[:, idx]
    a = queryq.T @ keysidxg
    p = np.exp(a - np.max(a, axis=1, keepdims=True))
    w = p * f64(size) / np.sum(p, axis=1, keepdims=True)
    wt = w.T
    vt = f64(vals)[:, idx].T
    equeryq = mxq(f64(equery), 0, "e4m3")
    ekeysidx2q = mxq(f64(ekeys)[:, idx2], 0, "e4m3")
    b = equeryq.T @ ekeysidx2q
    u1 = np.maximum(b - f64(th), 0.0) * f64(ew)
    ut = u1.T
    et = f64(evals)[:, idx2].T
    wtq = mxq(wt, 0, "e4m3")
    vtq = mxq(vt, 0, "e4m3")
    utq = mxq(ut, 0, "e4m3")
    etq = mxq(et, 0, "e4m3")
    o = wtq.T @ vtq + utq.T @ etq
    return o

@@ -1,0 +1,219 @@
+from contextlib import ExitStack
+
+import concourse.mybir as mybir
+from concourse.masks import make_identity
+
+D, T, I, Q, E, U, J = 512, 2048, 512, 128, 512, 1024, 512
+FLOPS = 2 * Q * (D * I + D * J + I * E + J * E)
+
+F32 = mybir.dt.float32
+BF16 = mybir.dt.bfloat16
+I32 = mybir.dt.int32
+U32 = mybir.dt.uint32
+U16 = mybir.dt.uint16
+U8 = mybir.dt.uint8
+FP8X4 = mybir.dt.float8_e4m3fn_x4
+ACT = mybir.ActivationFunctionType
+ALU = mybir.AluOpType
+AX = mybir.AxisListType
+
+P = 128
+PACK = 4
+BLOCKS = E // P
+WINDOW_BYTES = 4 * T
+TENANT_BYTES = 2048
+
+
+def tile_attend_editstore_kernel(tc, query, keys_words, keys_scales, size, vals, equery, ekeys, evals, th, ew, offs, offs2, out):
+    nc = tc.nc
+    with ExitStack() as ctx:
+        keep = ctx.enter_context(tc.tile_pool(name="keep", bufs=1))
+        shared = ctx.enter_context(tc.tile_pool(name="shared", bufs=1))
+        psum = ctx.enter_context(tc.psum_pool(name="psum", bufs=1))
+
+        place = {}
+
+        def kept(name, shape, dtype):
+            return keep.tile(shape, dtype, name=name, align_bytes=64)
+
+        def window(name, shape, dtype):
+            place[name] = len(place) * WINDOW_BYTES
+            return shared.tile(shape, dtype, name=name, align_bytes=64, offset=place[name])
+
+        def tenant(name, shape, dtype, of, part=0):
+            return shared.tile(shape, dtype, name=name, align_bytes=64, offset=place[of] + part * TENANT_BYTES)
+
+        def quantize(name, grouped, words, of=None, part=0):
+            if of is None:
+                codes = kept(name + "_codes", [P, words], U32)
+            else:
+                codes = tenant(name + "_codes", [P, words], U32, of, part)
+            scales = kept(name + "_scales", [P, words], U8)
+            nc.vector.quantize_mx(out=codes[:].bitcast(FP8X4), scales=scales[:], in_=grouped)
+            return codes, scales
+
+        def columns(operand, start, count):
+            return operand[0][:, start : start + count], operand[1][:, start : start + count]
+
+        def product(acc, stationary, moving, start, stop):
+            nc.tensor.matmul_mx(
+                out=acc,
+                lhsT=stationary[0][:].bitcast(FP8X4),
+                lhsT_scale=stationary[1][:],
+                rhs=moving[0][:].bitcast(FP8X4),
+                rhs_scale=moving[1][:],
+                start=start,
+                stop=stop,
+            )
+
+        slots = kept("slots", [P, I // 16], U16)
+        edits = kept("edits", [P, J // 16], U16)
+        key_words = kept("key_words", [P, T], I32)
+        key_bytes = kept("key_bytes", [P, T], U8)
+        q_raw = kept("q_raw", [P, PACK, Q], F32)
+        eq_raw = kept("eq_raw", [P, PACK, Q], F32)
+        ek_raw = [window("ek_raw%d" % h, [P, 2, U], F32) for h in range(2)]
+        ek_bf = [window("ek_bf%d" % h, [P, 2 * U], BF16) for h in range(2)]
+        ev_raw = [window("ev_raw%d" % b, [P, U], F32) for b in range(BLOCKS)]
+        v_raw = [window("v_raw%d" % b, [P, T], F32) for b in range(BLOCKS)]
+        size_col = kept("size_col", [P, PACK], F32)
+        ew_col = kept("ew_col", [P, PACK], F32)
+        th_col = kept("th_col", [P, 1], F32)
+        ident = kept("ident", [P, P], F32)
+
+        ek_pairs = ekeys.rearrange("(p h s) u -> h p s u", h=2, s=2)
+
+        def load_rows(tile, rows, b):
+            nc.sync.dma_start(tile[:], rows[b * P : (b + 1) * P, :])
+
+        nc.gpsimd.memset(key_bytes[:].bitcast(I32), 0)
+        nc.sync.dma_start(slots[:], offs)
+        nc.sync.dma_start(edits[:], offs2)
+        nc.sync.dma_start(key_words[:], keys_words[0].rearrange("p n t -> p (n t)").bitcast(I32))
+        for quad in range(4):
+            nc.scalar.dma_start(
+                key_bytes[32 * quad : 32 * quad + 4, :].bitcast(I32),
+                keys_scales[0, 4 * quad : 4 * quad + 4, :].bitcast(I32),
+            )
+        nc.sync.dma_start(q_raw[:], query.rearrange("(p t) q -> p t q", t=PACK))
+        nc.sync.dma_start(ek_raw[0][:], ek_pairs[0])
+        load_rows(ev_raw[0], evals, 0)
+        load_rows(ev_raw[1], evals, 1)
+        nc.sync.dma_start(size_col[:], size.rearrange("o (p t) -> (o p) t", t=PACK))
+        nc.sync.dma_start(ek_raw[1][:], ek_pairs[1])
+        nc.sync.dma_start(eq_raw[:], equery.rearrange("(p t) q -> p t q", t=PACK))
+        load_rows(ev_raw[2], evals, 2)
+        nc.sync.dma_start(th_col[:], th)
+        nc.sync.dma_start(ew_col[:], ew.rearrange("o (p t) -> (o p) t", t=PACK))
+        load_rows(ev_raw[3], evals, 3)
+        for b in range(BLOCKS):
+            load_rows(v_raw[b], vals, b)
+        make_identity(nc, ident[:])
+
+        def quantize_queries(name, raw):
+            grouped = kept(name + "_grouped", [P, Q, PACK], BF16)
+            nc.scalar.copy(grouped[:], raw[:].rearrange("p t q -> p q t"))
+            return quantize(name, grouped[:].rearrange("p q t -> p (q t)"), Q)
+
+        def turn_weights(name, rows, factor, tag, of):
+            turned = psum.tile([P, PACK, Q], F32, name=name + "_turned", tag=tag)
+            for t in range(PACK):
+                nc.tensor.transpose(turned[:, t, :], rows[:, t, :], ident[:])
+            grouped = tenant(name + "_grouped", [P, Q, PACK], BF16, of)
+            nc.vector.tensor_tensor(
+                grouped[:],
+                turned[:].rearrange("p t q -> p q t"),
+                factor[:].unsqueeze(1).to_broadcast([P, Q, PACK]),
+                ALU.mult,
+            )
+            return grouped[:].rearrange("p q t -> p (q t)")
+
+        def turn_values(name, raw, offsets, grouped):
+            picked = kept(name + "_picked", [P, I], BF16)
+            nc.vector.tensor_copy(picked[:], raw[:].indirect(offsets[:]))
+            pairs = picked[:].bitcast(F32)
+            turned = psum.tile([P, 2, P], F32, name=name + "_turned", tag="turned", bufs=2)
+            for h in range(2):
+                nc.tensor.transpose(turned[:, h, :], pairs[:, h::2], ident[:])
+            nc.scalar.copy(
+                grouped.bitcast(F32).rearrange("p (e h) -> p e h", h=2),
+                turned[:].rearrange("p h e -> p e h"),
+            )
+
+        def cast_edit_keys(h):
+            nc.scalar.activation(
+                ek_bf[h][:].rearrange("p (u s) -> p u s", s=2), ek_raw[h][:].rearrange("p s u -> p u s"), ACT.Copy
+            )
+
+        block = P * PACK
+        ev_grouped = kept("ev_grouped", [P, BLOCKS * block], BF16)
+        v_grouped = [kept("v_grouped%d" % g, [P, n * block], BF16) for g, n in enumerate((2, 1, 1))]
+        ek_picked = kept("ek_picked", [P, 2, J], F32)
+
+        k_codes = kept("k_codes", [P, I], U32)
+        k_scales = kept("k_scales", [P, I], U8)
+        nc.vector.tensor_copy(k_codes[:], key_words[:].bitcast(U32).indirect(slots[:]))
+        nc.vector.tensor_copy(k_scales[:], key_bytes[:].indirect(slots[:]))
+        q_mx = quantize_queries("q", q_raw)
+        scores = psum.tile([P, I], F32, name="scores", tag="attn")
+        product(scores[:], q_mx, (k_codes, k_scales), True, True)
+
+        neg_max = kept("neg_max", [P, 1], F32)
+        nc.vector.tensor_reduce(neg_max[:], scores[:], AX.X, ALU.max, negate=True)
+        cast_edit_keys(0)
+        p_rows = tenant("p_rows", [P, PACK, P], F32, "ek_raw0")
+        row_sum = kept("row_sum", [P, 1], F32)
+        nc.scalar.activation(
+            p_rows[:], scores[:].rearrange("q (p t) -> q t p", t=PACK), ACT.Exp, bias=neg_max[:], accum_out=row_sum[:]
+        )
+
+        turn_values("ev0", ev_raw[0], edits, ev_grouped[:, 0:block])
+        turn_values("ev1", ev_raw[1], edits, ev_grouped[:, block : 2 * block])
+
+        inv_sum = tenant("inv_sum", [P, 1], F32, "ev_raw1")
+        nc.vector.reciprocal(inv_sum[:], row_sum[:])
+        p_norm = kept("p_norm", [P, PACK, P], F32)
+        nc.scalar.activation(p_norm[:], p_rows[:], ACT.Copy, scale=inv_sum[:])
+
+        nc.vector.tensor_copy(ek_picked[:, 0, :], ek_bf[0][:].bitcast(F32).indirect(edits[:]))
+        w_grouped = turn_weights("w", p_norm, size_col, "attn", "ek_bf0")
+        cast_edit_keys(1)
+        turn_values("ev2", ev_raw[2], edits, ev_grouped[:, 2 * block : 3 * block])
+        w_mx = quantize("w", w_grouped, Q, "ev_raw2")
+        nc.vector.tensor_copy(ek_picked[:, 1, :], ek_bf[1][:].bitcast(F32).indirect(edits[:]))
+        ek_grouped = kept("ek_grouped", [P, J * PACK], BF16)
+        nc.scalar.copy(
+            ek_grouped[:].bitcast(F32).rearrange("p (j h) -> p j h", h=2), ek_picked[:].rearrange("p h j -> p j h")
+        )
+        turn_values("ev3", ev_raw[3], edits, ev_grouped[:, 3 * block : 4 * block])
+        eq_mx = quantize_queries("eq", eq_raw)
+        ek_mx = quantize("ek", ek_grouped[:], J, "ev_raw3")
+
+        turn_values("v0", v_raw[0], slots, v_grouped[0][:, 0:block])
+        ev_mx = quantize("ev", ev_grouped[:], BLOCKS * P, "v_raw0")
+        e_scores = psum.tile([P, J], F32, name="e_scores", tag="edit")
+        product(e_scores[:], eq_mx, ek_mx, True, True)
+        neg_th = kept("neg_th", [P, 1], F32)
+        nc.scalar.mul(neg_th[:], th_col[:], -1.0)
+        u_rows = kept("u_rows", [P, PACK, P], F32)
+        nc.scalar.activation(
+            u_rows[:], e_scores[:].rearrange("q (p t) -> q t p", t=PACK), ACT.Relu, bias=neg_th[:]
+        )
+
+        turn_values("v1", v_raw[1], slots, v_grouped[0][:, block : 2 * block])
+        u_grouped = turn_weights("u", u_rows, ew_col, "edit", "v_raw1")
+        turn_values("v2", v_raw[2], slots, v_grouped[1][:])
+        u_mx = quantize("u", u_grouped, Q, "v_raw2", 0)
+
+        def finish(name, v_mx, start, count):
+            acc = psum.tile([P, count], F32, name=name + "_acc")
+            product(acc[:], u_mx, columns(ev_mx, start, count), True, False)
+            product(acc[:], w_mx, v_mx, False, True)
+            result = kept(name + "_result", [P, count], F32)
+            nc.scalar.copy(result[:], acc[:])
+            nc.sync.dma_start(out[:, start : start + count], result[:])
+
+        finish("o01", quantize("v01", v_grouped[0][:], 2 * P, "v_raw2", 1), 0, 2 * P)
+        turn_values("v3", v_raw[3], slots, v_grouped[2][:])
+        finish("o2", quantize("v2", v_grouped[1][:], P, "v_raw3"), 2 * P, P)
+        finish("o3", quantize("v3", v_grouped[2][:], P), 3 * P, P)

@@ -20,8 +20,7 @@ AX = mybir.AxisListType
 P = 128
 PACK = 4
 BLOCKS = E // P
-WINDOW_BYTES = 4 * T
-TENANT_BYTES = 2048
+KIB = 1024
 
 
 def tile_attend_editstore_kernel(tc, query, keys_words, keys_scales, size, vals, equery, ekeys, evals, th, ew, offs, offs2, out):
@@ -32,22 +31,25 @@ def tile_attend_editstore_kernel(tc, query, keys_words, keys_scales, size, vals,
         psum = ctx.enter_context(tc.psum_pool(name="psum", bufs=1))
 
         place = {}
+        rooms = []
 
         def kept(name, shape, dtype):
             return keep.tile(shape, dtype, name=name, align_bytes=64)
 
-        def window(name, shape, dtype):
-            place[name] = len(place) * WINDOW_BYTES
+        def host(name, shape, dtype, room):
+            place[name] = sum(rooms)
+            rooms.append(room)
             return shared.tile(shape, dtype, name=name, align_bytes=64, offset=place[name])
 
-        def tenant(name, shape, dtype, of, part=0):
-            return shared.tile(shape, dtype, name=name, align_bytes=64, offset=place[of] + part * TENANT_BYTES)
+        def tenant(name, shape, dtype, of, at=0):
+            place[name] = place[of] + at
+            return shared.tile(shape, dtype, name=name, align_bytes=64, offset=place[name])
 
-        def quantize(name, grouped, words, of=None, part=0):
-            if of is None:
-                codes = kept(name + "_codes", [P, words], U32)
-            else:
-                codes = tenant(name + "_codes", [P, words], U32, of, part)
+        def fresh_or_tenant(name, shape, dtype, of, at):
+            return kept(name, shape, dtype) if of is None else tenant(name, shape, dtype, of, at)
+
+        def quantize(name, grouped, words, of=None, at=0):
+            codes = fresh_or_tenant(name + "_codes", [P, words], U32, of, at)
             scales = kept(name + "_scales", [P, words], U8)
             nc.vector.quantize_mx(out=codes[:].bitcast(FP8X4), scales=scales[:], in_=grouped)
             return codes, scales
@@ -68,14 +70,13 @@ def tile_attend_editstore_kernel(tc, query, keys_words, keys_scales, size, vals,
 
         slots = kept("slots", [P, I // 16], U16)
         edits = kept("edits", [P, J // 16], U16)
-        key_words = kept("key_words", [P, T], I32)
+        key_words = host("key_words", [P, T], I32, 8 * KIB)
+        q_raw = host("q_raw", [P, PACK, Q], F32, 2 * KIB)
         key_bytes = kept("key_bytes", [P, T], U8)
-        q_raw = kept("q_raw", [P, PACK, Q], F32)
         eq_raw = kept("eq_raw", [P, PACK, Q], F32)
-        ek_raw = [window("ek_raw%d" % h, [P, 2, U], F32) for h in range(2)]
-        ek_bf = [window("ek_bf%d" % h, [P, 2 * U], BF16) for h in range(2)]
-        ev_raw = [window("ev_raw%d" % b, [P, U], F32) for b in range(BLOCKS)]
-        v_raw = [window("v_raw%d" % b, [P, T], F32) for b in range(BLOCKS)]
+        ek_raw = [host("ek_raw%d" % h, [P, 2, U], F32, 8 * KIB) for h in range(2)]
+        ev_raw = [host("ev_raw%d" % b, [P, U], F32, 4 * KIB) for b in range(BLOCKS)]
+        v_raw = [host("v_raw%d" % b, [P, T], F32, 8 * KIB) for b in range(BLOCKS)]
         size_col = kept("size_col", [P, PACK], F32)
         ew_col = kept("ew_col", [P, PACK], F32)
         th_col = kept("th_col", [P, 1], F32)
@@ -96,13 +97,13 @@ def tile_attend_editstore_kernel(tc, query, keys_words, keys_scales, size, vals,
                 keys_scales[0, 4 * quad : 4 * quad + 4, :].bitcast(I32),
             )
         nc.sync.dma_start(q_raw[:], query.rearrange("(p t) q -> p t q", t=PACK))
-        nc.sync.dma_start(ek_raw[0][:], ek_pairs[0])
         load_rows(ev_raw[0], evals, 0)
+        nc.sync.dma_start(ek_raw[0][:], ek_pairs[0])
         load_rows(ev_raw[1], evals, 1)
         nc.sync.dma_start(size_col[:], size.rearrange("o (p t) -> (o p) t", t=PACK))
+        load_rows(ev_raw[2], evals, 2)
         nc.sync.dma_start(ek_raw[1][:], ek_pairs[1])
         nc.sync.dma_start(eq_raw[:], equery.rearrange("(p t) q -> p t q", t=PACK))
-        load_rows(ev_raw[2], evals, 2)
         nc.sync.dma_start(th_col[:], th)
         nc.sync.dma_start(ew_col[:], ew.rearrange("o (p t) -> (o p) t", t=PACK))
         load_rows(ev_raw[3], evals, 3)
@@ -110,16 +111,15 @@ def tile_attend_editstore_kernel(tc, query, keys_words, keys_scales, size, vals,
             load_rows(v_raw[b], vals, b)
         make_identity(nc, ident[:])
 
-        def quantize_queries(name, raw):
-            grouped = kept(name + "_grouped", [P, Q, PACK], BF16)
+        def group_queries(raw, grouped):
             nc.scalar.copy(grouped[:], raw[:].rearrange("p t q -> p q t"))
-            return quantize(name, grouped[:].rearrange("p q t -> p (q t)"), Q)
+            return grouped[:].rearrange("p q t -> p (q t)")
 
-        def turn_weights(name, rows, factor, tag, of):
-            turned = psum.tile([P, PACK, Q], F32, name=name + "_turned", tag=tag)
+        def turn_weights(name, rows, factor, bank):
+            turned = psum.tile([P, PACK, Q], F32, name=name + "_turned", tag=bank)
             for t in range(PACK):
                 nc.tensor.transpose(turned[:, t, :], rows[:, t, :], ident[:])
-            grouped = tenant(name + "_grouped", [P, Q, PACK], BF16, of)
+            grouped = kept(name + "_grouped", [P, Q, PACK], BF16)
             nc.vector.tensor_tensor(
                 grouped[:],
                 turned[:].rearrange("p t q -> p q t"),
@@ -128,11 +128,14 @@ def tile_attend_editstore_kernel(tc, query, keys_words, keys_scales, size, vals,
             )
             return grouped[:].rearrange("p q t -> p (q t)")
 
-        def turn_values(name, raw, offsets, grouped):
-            picked = kept(name + "_picked", [P, I], BF16)
+        def pick_values(name, raw, offsets, of, at=0):
+            picked = tenant(name + "_picked", [P, I], BF16, of, at)
             nc.vector.tensor_copy(picked[:], raw[:].indirect(offsets[:]))
+            return picked
+
+        def turn_values(name, picked, grouped, bank):
             pairs = picked[:].bitcast(F32)
-            turned = psum.tile([P, 2, P], F32, name=name + "_turned", tag="turned", bufs=2)
+            turned = psum.tile([P, 2, P], F32, name=name + "_turned", tag=bank)
             for h in range(2):
                 nc.tensor.transpose(turned[:, h, :], pairs[:, h::2], ident[:])
             nc.scalar.copy(
@@ -140,80 +143,102 @@ def tile_attend_editstore_kernel(tc, query, keys_words, keys_scales, size, vals,
                 turned[:].rearrange("p h e -> p e h"),
             )
 
-        def cast_edit_keys(h):
+        def cast_edit_keys(paired, raw):
             nc.scalar.activation(
-                ek_bf[h][:].rearrange("p (u s) -> p u s", s=2), ek_raw[h][:].rearrange("p s u -> p u s"), ACT.Copy
+                paired[:].rearrange("p (u s) -> p u s", s=2), raw[:].rearrange("p s u -> p u s"), ACT.Copy
             )
 
         block = P * PACK
-        ev_grouped = kept("ev_grouped", [P, BLOCKS * block], BF16)
-        v_grouped = [kept("v_grouped%d" % g, [P, n * block], BF16) for g, n in enumerate((2, 1, 1))]
-        ek_picked = kept("ek_picked", [P, 2, J], F32)
 
-        k_codes = kept("k_codes", [P, I], U32)
+        k_codes = host("k_codes", [P, I], U32, 2 * KIB)
         k_scales = kept("k_scales", [P, I], U8)
-        nc.vector.tensor_copy(k_codes[:], key_words[:].bitcast(U32).indirect(slots[:]))
         nc.vector.tensor_copy(k_scales[:], key_bytes[:].indirect(slots[:]))
-        q_mx = quantize_queries("q", q_raw)
+        nc.vector.tensor_copy(k_codes[:], key_words[:].bitcast(U32).indirect(slots[:]))
+        q_grouped = kept("q_grouped", [P, Q, PACK], BF16)
+        q_mx = quantize("q", group_queries(q_raw, q_grouped), Q, "key_words")
         scores = psum.tile([P, I], F32, name="scores", tag="attn")
         product(scores[:], q_mx, (k_codes, k_scales), True, True)
 
-        neg_max = kept("neg_max", [P, 1], F32)
-        nc.vector.tensor_reduce(neg_max[:], scores[:], AX.X, ALU.max, negate=True)
-        cast_edit_keys(0)
-        p_rows = tenant("p_rows", [P, PACK, P], F32, "ek_raw0")
-        row_sum = kept("row_sum", [P, 1], F32)
+        ev_picked0 = pick_values("ev0", ev_raw[0], edits, "q_raw", -KIB // 2)
+        rooms.append(KIB)
+        max_line = host("max_line", [P, 32], F32, 5 * KIB)
+        neg_max = max_line[:, 0:1]
+        nc.vector.tensor_reduce(neg_max, scores[:], AX.X, ALU.max, negate=True)
+        p_rows = kept("p_rows", [P, PACK, P], F32)
+        row_sum = host("row_sum", [P, 1], F32, 4 * KIB)
         nc.scalar.activation(
-            p_rows[:], scores[:].rearrange("q (p t) -> q t p", t=PACK), ACT.Exp, bias=neg_max[:], accum_out=row_sum[:]
+            p_rows[:], scores[:].rearrange("q (p t) -> q t p", t=PACK), ACT.Exp, bias=neg_max, accum_out=row_sum[:]
         )
+        ek_paired0 = tenant("ek_paired0", [P, 2 * U], BF16, "max_line", 64)
+        cast_edit_keys(ek_paired0, ek_raw[0])
 
-        turn_values("ev0", ev_raw[0], edits, ev_grouped[:, 0:block])
-        turn_values("ev1", ev_raw[1], edits, ev_grouped[:, block : 2 * block])
-
-        inv_sum = tenant("inv_sum", [P, 1], F32, "ev_raw1")
+        ev_picked1 = pick_values("ev1", ev_raw[1], edits, "k_codes")
+        inv_sum = kept("inv_sum", [P, 1], F32)
         nc.vector.reciprocal(inv_sum[:], row_sum[:])
-        p_norm = kept("p_norm", [P, PACK, P], F32)
+        p_norm = host("p_norm", [P, PACK, P], F32, 2 * KIB)
         nc.scalar.activation(p_norm[:], p_rows[:], ACT.Copy, scale=inv_sum[:])
+        ev_grouped0 = tenant("ev_grouped0", [P, 2 * block], BF16, "ek_raw0")
+        turn_values("ev0", ev_picked0, ev_grouped0[:, 0:block], "even")
+        turn_values("ev1", ev_picked1, ev_grouped0[:, block : 2 * block], "odd")
 
-        nc.vector.tensor_copy(ek_picked[:, 0, :], ek_bf[0][:].bitcast(F32).indirect(edits[:]))
-        w_grouped = turn_weights("w", p_norm, size_col, "attn", "ek_bf0")
-        cast_edit_keys(1)
-        turn_values("ev2", ev_raw[2], edits, ev_grouped[:, 2 * block : 3 * block])
-        w_mx = quantize("w", w_grouped, Q, "ev_raw2")
-        nc.vector.tensor_copy(ek_picked[:, 1, :], ek_bf[1][:].bitcast(F32).indirect(edits[:]))
+        ev_picked2 = pick_values("ev2", ev_raw[2], edits, "max_line", 64 - KIB)
+        ek_picked = host("ek_picked", [P, 2, J], F32, 4 * KIB)
+        nc.vector.tensor_copy(ek_picked[:, 0, :], ek_paired0[:].bitcast(F32).indirect(edits[:]))
+        ev_mx0 = quantize("ev0", ev_grouped0[:], 2 * P)
+        w_grouped = turn_weights("w", p_norm, size_col, "attn")
+
+        ek_paired1 = tenant("ek_paired1", [P, 2 * U], BF16, "row_sum")
+        cast_edit_keys(ek_paired1, ek_raw[1])
+        eq_grouped = tenant("eq_grouped", [P, Q, PACK], BF16, "ek_raw1")
+        eq_words = group_queries(eq_raw, eq_grouped)
+        ev_grouped1 = tenant("ev_grouped1", [P, 2 * block], BF16, "ek_raw1", 4 * KIB)
+        turn_values("ev2", ev_picked2, ev_grouped1[:, 0:block], "even")
+        ev_picked3 = pick_values("ev3", ev_raw[3], edits, "p_norm")
+        turn_values("ev3", ev_picked3, ev_grouped1[:, block : 2 * block], "odd")
+
+        nc.vector.tensor_copy(ek_picked[:, 1, :], ek_paired1[:].bitcast(F32).indirect(edits[:]))
         ek_grouped = kept("ek_grouped", [P, J * PACK], BF16)
         nc.scalar.copy(
             ek_grouped[:].bitcast(F32).rearrange("p (j h) -> p j h", h=2), ek_picked[:].rearrange("p h j -> p j h")
         )
-        turn_values("ev3", ev_raw[3], edits, ev_grouped[:, 3 * block : 4 * block])
-        eq_mx = quantize_queries("eq", eq_raw)
-        ek_mx = quantize("ek", ek_grouped[:], J, "ev_raw3")
-
-        turn_values("v0", v_raw[0], slots, v_grouped[0][:, 0:block])
-        ev_mx = quantize("ev", ev_grouped[:], BLOCKS * P, "v_raw0")
+        w_mx = quantize("w", w_grouped, Q)
+        eq_mx = quantize("eq", eq_words, Q)
+        v_picked0 = pick_values("v0", v_raw[0], slots, "ek_raw1", 6 * KIB)
+        rooms.append(2 * KIB)
+        place["ek_room"] = sum(rooms) - 2 * KIB
+        ek_mx = quantize("ek", ek_grouped[:], J, "ek_room")
         e_scores = psum.tile([P, J], F32, name="e_scores", tag="edit")
         product(e_scores[:], eq_mx, ek_mx, True, True)
-        neg_th = kept("neg_th", [P, 1], F32)
+        neg_th = tenant("neg_th", [P, 1], F32, "ek_raw1", KIB)
         nc.scalar.mul(neg_th[:], th_col[:], -1.0)
-        u_rows = kept("u_rows", [P, PACK, P], F32)
+        u_rows = host("u_rows", [P, PACK, P], F32, 2 * KIB)
         nc.scalar.activation(
             u_rows[:], e_scores[:].rearrange("q (p t) -> q t p", t=PACK), ACT.Relu, bias=neg_th[:]
         )
 
-        turn_values("v1", v_raw[1], slots, v_grouped[0][:, block : 2 * block])
-        u_grouped = turn_weights("u", u_rows, ew_col, "edit", "v_raw1")
-        turn_values("v2", v_raw[2], slots, v_grouped[1][:])
-        u_mx = quantize("u", u_grouped, Q, "v_raw2", 0)
+        v_grouped01 = tenant("v_grouped01", [P, 2 * block], BF16, "neg_th")
+        v_grouped2 = kept("v_grouped2", [P, block], BF16)
+        v_grouped3 = kept("v_grouped3", [P, block], BF16)
+        turn_values("v0", v_picked0, v_grouped01[:, 0:block], "even")
+        ev_mx1 = quantize("ev1", ev_grouped1[:], 2 * P)
 
-        def finish(name, v_mx, start, count):
+        v_picked1 = pick_values("v1", v_raw[1], slots, "ek_picked")
+        v_picked2 = pick_values("v2", v_raw[2], slots, "ek_codes")
+        u_grouped = turn_weights("u", u_rows, ew_col, "edit")
+        turn_values("v1", v_picked1, v_grouped01[:, block : 2 * block], "odd")
+        turn_values("v2", v_picked2, v_grouped2[:], "edit")
+        v_picked3 = pick_values("v3", v_raw[3], slots, "u_rows")
+        turn_values("v3", v_picked3, v_grouped3[:], "even")
+        u_mx = quantize("u", u_grouped, Q, "v_raw3")
+
+        def finish(name, ev_mx, v_mx, start, count):
             acc = psum.tile([P, count], F32, name=name + "_acc")
-            product(acc[:], u_mx, columns(ev_mx, start, count), True, False)
+            product(acc[:], u_mx, ev_mx, True, False)
             product(acc[:], w_mx, v_mx, False, True)
             result = kept(name + "_result", [P, count], F32)
             nc.scalar.copy(result[:], acc[:])
             nc.sync.dma_start(out[:, start : start + count], result[:])
 
-        finish("o01", quantize("v01", v_grouped[0][:], 2 * P, "v_raw2", 1), 0, 2 * P)
-        turn_values("v3", v_raw[3], slots, v_grouped[2][:])
-        finish("o2", quantize("v2", v_grouped[1][:], P, "v_raw3"), 2 * P, P)
-        finish("o3", quantize("v3", v_grouped[2][:], P), 3 * P, P)
+        finish("o01", ev_mx0, quantize("v01", v_grouped01[:], 2 * P, "v_raw3", KIB), 0, 2 * P)
+        finish("o2", columns(ev_mx1, 0, P), quantize("v2", v_grouped2[:], P, "v_raw3", 2 * KIB), 2 * P, P)
+        finish("o3", columns(ev_mx1, P, P), quantize("v3", v_grouped3[:], P), 3 * P, P)

@@ -70,12 +70,12 @@ def tile_attend_editstore_kernel(tc, query, keys_words, keys_scales, size, vals,
 
         slots = kept("slots", [P, I // 16], U16)
         edits = kept("edits", [P, J // 16], U16)
-        key_words = host("key_words", [P, T], I32, 8 * KIB)
-        q_raw = host("q_raw", [P, PACK, Q], F32, 2 * KIB)
+        key_words = kept("key_words", [P, T], I32)
         key_bytes = kept("key_bytes", [P, T], U8)
+        q_raw = kept("q_raw", [P, PACK, Q], F32)
         eq_raw = kept("eq_raw", [P, PACK, Q], F32)
         ek_raw = [host("ek_raw%d" % h, [P, 2, U], F32, 8 * KIB) for h in range(2)]
-        ev_raw = [host("ev_raw%d" % b, [P, U], F32, 4 * KIB) for b in range(BLOCKS)]
+        ev_raw = [kept("ev_raw%d" % b, [P, U], F32) for b in range(BLOCKS)]
         v_raw = [host("v_raw%d" % b, [P, T], F32, 8 * KIB) for b in range(BLOCKS)]
         size_col = kept("size_col", [P, PACK], F32)
         ew_col = kept("ew_col", [P, PACK], F32)
@@ -90,21 +90,21 @@ def tile_attend_editstore_kernel(tc, query, keys_words, keys_scales, size, vals,
         nc.gpsimd.memset(key_bytes[:].bitcast(I32), 0)
         nc.sync.dma_start(slots[:], offs)
         nc.sync.dma_start(edits[:], offs2)
-        nc.sync.dma_start(key_words[:], keys_words[0].rearrange("p n t -> p (n t)").bitcast(I32))
+        nc.sync.dma_start(q_raw[:], query.rearrange("(p t) q -> p t q", t=PACK))
+        nc.sync.dma_start(eq_raw[:], equery.rearrange("(p t) q -> p t q", t=PACK))
         for quad in range(4):
             nc.scalar.dma_start(
                 key_bytes[32 * quad : 32 * quad + 4, :].bitcast(I32),
                 keys_scales[0, 4 * quad : 4 * quad + 4, :].bitcast(I32),
             )
-        nc.sync.dma_start(q_raw[:], query.rearrange("(p t) q -> p t q", t=PACK))
-        load_rows(ev_raw[0], evals, 0)
+        nc.sync.dma_start(key_words[:], keys_words[0].rearrange("p n t -> p (n t)").bitcast(I32))
         nc.sync.dma_start(ek_raw[0][:], ek_pairs[0])
+        load_rows(ev_raw[0], evals, 0)
+        nc.sync.dma_start(th_col[:], th)
+        nc.sync.dma_start(ek_raw[1][:], ek_pairs[1])
         load_rows(ev_raw[1], evals, 1)
         nc.sync.dma_start(size_col[:], size.rearrange("o (p t) -> (o p) t", t=PACK))
         load_rows(ev_raw[2], evals, 2)
-        nc.sync.dma_start(ek_raw[1][:], ek_pairs[1])
-        nc.sync.dma_start(eq_raw[:], equery.rearrange("(p t) q -> p t q", t=PACK))
-        nc.sync.dma_start(th_col[:], th)
         nc.sync.dma_start(ew_col[:], ew.rearrange("o (p t) -> (o p) t", t=PACK))
         load_rows(ev_raw[3], evals, 3)
         for b in range(BLOCKS):
@@ -115,11 +115,11 @@ def tile_attend_editstore_kernel(tc, query, keys_words, keys_scales, size, vals,
             nc.scalar.copy(grouped[:], raw[:].rearrange("p t q -> p q t"))
             return grouped[:].rearrange("p q t -> p (q t)")
 
-        def turn_weights(name, rows, factor, bank):
+        def turn_weights(name, rows, factor, bank, of=None):
             turned = psum.tile([P, PACK, Q], F32, name=name + "_turned", tag=bank)
             for t in range(PACK):
                 nc.tensor.transpose(turned[:, t, :], rows[:, t, :], ident[:])
-            grouped = kept(name + "_grouped", [P, Q, PACK], BF16)
+            grouped = fresh_or_tenant(name + "_grouped", [P, Q, PACK], BF16, of, 0)
             nc.vector.tensor_tensor(
                 grouped[:],
                 turned[:].rearrange("p t q -> p q t"),
@@ -128,8 +128,8 @@ def tile_attend_editstore_kernel(tc, query, keys_words, keys_scales, size, vals,
             )
             return grouped[:].rearrange("p q t -> p (q t)")
 
-        def pick_values(name, raw, offsets, of, at=0):
-            picked = tenant(name + "_picked", [P, I], BF16, of, at)
+        def pick_values(name, raw, offsets, of=None, at=0):
+            picked = fresh_or_tenant(name + "_picked", [P, I], BF16, of, at)
             nc.vector.tensor_copy(picked[:], raw[:].indirect(offsets[:]))
             return picked
 
@@ -150,86 +150,77 @@ def tile_attend_editstore_kernel(tc, query, keys_words, keys_scales, size, vals,
 
         block = P * PACK
 
-        k_codes = host("k_codes", [P, I], U32, 2 * KIB)
+        k_codes = kept("k_codes", [P, I], U32)
         k_scales = kept("k_scales", [P, I], U8)
         nc.vector.tensor_copy(k_scales[:], key_bytes[:].indirect(slots[:]))
-        nc.vector.tensor_copy(k_codes[:], key_words[:].bitcast(U32).indirect(slots[:]))
         q_grouped = kept("q_grouped", [P, Q, PACK], BF16)
-        q_mx = quantize("q", group_queries(q_raw, q_grouped), Q, "key_words")
+        q_mx = quantize("q", group_queries(q_raw, q_grouped), Q)
+        eq_grouped = kept("eq_grouped", [P, Q, PACK], BF16)
+        eq_mx = quantize("eq", group_queries(eq_raw, eq_grouped), Q)
+        nc.vector.tensor_copy(k_codes[:], key_words[:].bitcast(U32).indirect(slots[:]))
         scores = psum.tile([P, I], F32, name="scores", tag="attn")
         product(scores[:], q_mx, (k_codes, k_scales), True, True)
 
-        ev_picked0 = pick_values("ev0", ev_raw[0], edits, "q_raw", -KIB // 2)
-        rooms.append(KIB)
-        max_line = host("max_line", [P, 32], F32, 5 * KIB)
-        neg_max = max_line[:, 0:1]
-        nc.vector.tensor_reduce(neg_max, scores[:], AX.X, ALU.max, negate=True)
-        p_rows = kept("p_rows", [P, PACK, P], F32)
-        row_sum = host("row_sum", [P, 1], F32, 4 * KIB)
+        neg_max = kept("neg_max", [P, 1], F32)
+        nc.vector.tensor_reduce(neg_max[:], scores[:], AX.X, ALU.max, negate=True)
+        ek_paired = [kept("ek_paired%d" % h, [P, 2 * U], BF16) for h in range(2)]
+        cast_edit_keys(ek_paired[0], ek_raw[0])
+        p_rows = tenant("p_rows", [P, PACK, P], F32, "ek_raw0")
+        row_sum = kept("row_sum", [P, 1], F32)
         nc.scalar.activation(
-            p_rows[:], scores[:].rearrange("q (p t) -> q t p", t=PACK), ACT.Exp, bias=neg_max, accum_out=row_sum[:]
+            p_rows[:], scores[:].rearrange("q (p t) -> q t p", t=PACK), ACT.Exp, bias=neg_max[:], accum_out=row_sum[:]
         )
-        ek_paired0 = tenant("ek_paired0", [P, 2 * U], BF16, "max_line", 64)
-        cast_edit_keys(ek_paired0, ek_raw[0])
 
-        ev_picked1 = pick_values("ev1", ev_raw[1], edits, "k_codes")
+        ev_picked0 = pick_values("ev0", ev_raw[0], edits)
+        ek_picked = host("ek_picked", [P, 2, J], F32, 4 * KIB)
+        nc.vector.tensor_copy(ek_picked[:, 0, :], ek_paired[0][:].bitcast(F32).indirect(edits[:]))
         inv_sum = kept("inv_sum", [P, 1], F32)
         nc.vector.reciprocal(inv_sum[:], row_sum[:])
-        p_norm = host("p_norm", [P, PACK, P], F32, 2 * KIB)
+        cast_edit_keys(ek_paired[1], ek_raw[1])
+        p_norm = tenant("p_norm", [P, PACK, P], F32, "ek_raw1")
         nc.scalar.activation(p_norm[:], p_rows[:], ACT.Copy, scale=inv_sum[:])
-        ev_grouped0 = tenant("ev_grouped0", [P, 2 * block], BF16, "ek_raw0")
+        ev_grouped0 = tenant("ev_grouped0", [P, 2 * block], BF16, "ek_raw1", 2 * KIB)
         turn_values("ev0", ev_picked0, ev_grouped0[:, 0:block], "even")
+        ev_picked1 = pick_values("ev1", ev_raw[1], edits)
         turn_values("ev1", ev_picked1, ev_grouped0[:, block : 2 * block], "odd")
 
-        ev_picked2 = pick_values("ev2", ev_raw[2], edits, "max_line", 64 - KIB)
-        ek_picked = host("ek_picked", [P, 2, J], F32, 4 * KIB)
-        nc.vector.tensor_copy(ek_picked[:, 0, :], ek_paired0[:].bitcast(F32).indirect(edits[:]))
-        ev_mx0 = quantize("ev0", ev_grouped0[:], 2 * P)
-        w_grouped = turn_weights("w", p_norm, size_col, "attn")
-
-        ek_paired1 = tenant("ek_paired1", [P, 2 * U], BF16, "row_sum")
-        cast_edit_keys(ek_paired1, ek_raw[1])
-        eq_grouped = tenant("eq_grouped", [P, Q, PACK], BF16, "ek_raw1")
-        eq_words = group_queries(eq_raw, eq_grouped)
-        ev_grouped1 = tenant("ev_grouped1", [P, 2 * block], BF16, "ek_raw1", 4 * KIB)
-        turn_values("ev2", ev_picked2, ev_grouped1[:, 0:block], "even")
-        ev_picked3 = pick_values("ev3", ev_raw[3], edits, "p_norm")
-        turn_values("ev3", ev_picked3, ev_grouped1[:, block : 2 * block], "odd")
-
-        nc.vector.tensor_copy(ek_picked[:, 1, :], ek_paired1[:].bitcast(F32).indirect(edits[:]))
+        nc.vector.tensor_copy(ek_picked[:, 1, :], ek_paired[1][:].bitcast(F32).indirect(edits[:]))
         ek_grouped = kept("ek_grouped", [P, J * PACK], BF16)
         nc.scalar.copy(
             ek_grouped[:].bitcast(F32).rearrange("p (j h) -> p j h", h=2), ek_picked[:].rearrange("p h j -> p j h")
         )
-        w_mx = quantize("w", w_grouped, Q)
-        eq_mx = quantize("eq", eq_words, Q)
-        v_picked0 = pick_values("v0", v_raw[0], slots, "ek_raw1", 6 * KIB)
-        rooms.append(2 * KIB)
-        place["ek_room"] = sum(rooms) - 2 * KIB
-        ek_mx = quantize("ek", ek_grouped[:], J, "ek_room")
+        ev_picked2 = pick_values("ev2", ev_raw[2], edits, "ek_raw1", 4 * KIB)
+        w_grouped = turn_weights("w", p_norm, size_col, "attn")
+        ek_mx = quantize("ek", ek_grouped[:], J)
         e_scores = psum.tile([P, J], F32, name="e_scores", tag="edit")
         product(e_scores[:], eq_mx, ek_mx, True, True)
-        neg_th = tenant("neg_th", [P, 1], F32, "ek_raw1", KIB)
+        neg_th = tenant("neg_th", [P, 1], F32, "ek_raw1", 5 * KIB)
         nc.scalar.mul(neg_th[:], th_col[:], -1.0)
-        u_rows = host("u_rows", [P, PACK, P], F32, 2 * KIB)
+        u_rows = kept("u_rows", [P, PACK, P], F32)
         nc.scalar.activation(
             u_rows[:], e_scores[:].rearrange("q (p t) -> q t p", t=PACK), ACT.Relu, bias=neg_th[:]
         )
+        ev_grouped1 = kept("ev_grouped1", [P, 2 * block], BF16)
+        turn_values("ev2", ev_picked2, ev_grouped1[:, 0:block], "attn")
+        ev_picked3 = pick_values("ev3", ev_raw[3], edits, "ek_picked")
+        turn_values("ev3", ev_picked3, ev_grouped1[:, block : 2 * block], "even")
+        ev_mx0 = quantize("ev0", ev_grouped0[:], 2 * P)
 
         v_grouped01 = tenant("v_grouped01", [P, 2 * block], BF16, "neg_th")
         v_grouped2 = kept("v_grouped2", [P, block], BF16)
         v_grouped3 = kept("v_grouped3", [P, block], BF16)
-        turn_values("v0", v_picked0, v_grouped01[:, 0:block], "even")
-        ev_mx1 = quantize("ev1", ev_grouped1[:], 2 * P)
-
-        v_picked1 = pick_values("v1", v_raw[1], slots, "ek_picked")
-        v_picked2 = pick_values("v2", v_raw[2], slots, "ek_codes")
-        u_grouped = turn_weights("u", u_rows, ew_col, "edit")
+        v_picked0 = pick_values("v0", v_raw[0], slots)
+        v_picked1 = pick_values("v1", v_raw[1], slots)
+        u_grouped = turn_weights("u", u_rows, ew_col, "edit", "v_raw1")
+        turn_values("v0", v_picked0, v_grouped01[:, 0:block], "edit")
         turn_values("v1", v_picked1, v_grouped01[:, block : 2 * block], "odd")
-        turn_values("v2", v_picked2, v_grouped2[:], "edit")
-        v_picked3 = pick_values("v3", v_raw[3], slots, "u_rows")
-        turn_values("v3", v_picked3, v_grouped3[:], "even")
+        v_picked2 = pick_values("v2", v_raw[2], slots)
+        turn_values("v2", v_picked2, v_grouped2[:], "even")
+        v_picked3 = pick_values("v3", v_raw[3], slots)
+        turn_values("v3", v_picked3, v_grouped3[:], "odd")
         u_mx = quantize("u", u_grouped, Q, "v_raw3")
+        w_mx = quantize("w", w_grouped, Q, "v_raw3", 3 * KIB)
+        ev_mx1 = quantize("ev1", ev_grouped1[:], 2 * P, "v_raw3", 4 * KIB)
 
         def finish(name, ev_mx, v_mx, start, count):
             acc = psum.tile([P, count], F32, name=name + "_acc")

from contextlib import ExitStack

import concourse.mybir as mybir
from concourse.masks import make_identity

D, T, I, Q, E, U, J = 512, 2048, 512, 128, 512, 1024, 512
FLOPS = 2 * Q * (D * I + D * J + I * E + J * E)

F32 = mybir.dt.float32
BF16 = mybir.dt.bfloat16
I32 = mybir.dt.int32
U32 = mybir.dt.uint32
U16 = mybir.dt.uint16
U8 = mybir.dt.uint8
FP8X4 = mybir.dt.float8_e4m3fn_x4
ACT = mybir.ActivationFunctionType
ALU = mybir.AluOpType
AX = mybir.AxisListType

P = 128
PACK = 4
BLOCKS = E // P
KIB = 1024


def tile_attend_editstore_kernel(tc, query, keys_words, keys_scales, size, vals, equery, ekeys, evals, th, ew, offs, offs2, out):
    nc = tc.nc
    with ExitStack() as ctx:
        keep = ctx.enter_context(tc.tile_pool(name="keep", bufs=1))
        shared = ctx.enter_context(tc.tile_pool(name="shared", bufs=1))
        psum = ctx.enter_context(tc.psum_pool(name="psum", bufs=1))

        place = {}
        rooms = []

        def kept(name, shape, dtype):
            return keep.tile(shape, dtype, name=name, align_bytes=64)

        def host(name, shape, dtype, room):
            place[name] = sum(rooms)
            rooms.append(room)
            return shared.tile(shape, dtype, name=name, align_bytes=64, offset=place[name])

        def tenant(name, shape, dtype, of, at=0):
            place[name] = place[of] + at
            return shared.tile(shape, dtype, name=name, align_bytes=64, offset=place[name])

        def fresh_or_tenant(name, shape, dtype, of, at):
            return kept(name, shape, dtype) if of is None else tenant(name, shape, dtype, of, at)

        def quantize(name, grouped, words, of=None, at=0):
            codes = fresh_or_tenant(name + "_codes", [P, words], U32, of, at)
            scales = kept(name + "_scales", [P, words], U8)
            nc.vector.quantize_mx(out=codes[:].bitcast(FP8X4), scales=scales[:], in_=grouped)
            return codes, scales

        def columns(operand, start, count):
            return operand[0][:, start : start + count], operand[1][:, start : start + count]

        def product(acc, stationary, moving, start, stop):
            nc.tensor.matmul_mx(
                out=acc,
                lhsT=stationary[0][:].bitcast(FP8X4),
                lhsT_scale=stationary[1][:],
                rhs=moving[0][:].bitcast(FP8X4),
                rhs_scale=moving[1][:],
                start=start,
                stop=stop,
            )

        slots = kept("slots", [P, I // 16], U16)
        edits = kept("edits", [P, J // 16], U16)
        key_words = kept("key_words", [P, T], I32)
        key_bytes = kept("key_bytes", [P, T], U8)
        q_raw = kept("q_raw", [P, PACK, Q], F32)
        eq_raw = kept("eq_raw", [P, PACK, Q], F32)
        ek_raw = [host("ek_raw%d" % h, [P, 2, U], F32, 8 * KIB) for h in range(2)]
        ev_raw = [kept("ev_raw%d" % b, [P, U], F32) for b in range(BLOCKS)]
        v_raw = [host("v_raw%d" % b, [P, T], F32, 8 * KIB) for b in range(BLOCKS)]
        size_col = kept("size_col", [P, PACK], F32)
        ew_col = kept("ew_col", [P, PACK], F32)
        th_col = kept("th_col", [P, 1], F32)
        ident = kept("ident", [P, P], F32)

        ek_pairs = ekeys.rearrange("(p h s) u -> h p s u", h=2, s=2)

        def load_rows(tile, rows, b):
            nc.sync.dma_start(tile[:], rows[b * P : (b + 1) * P, :])

        nc.gpsimd.memset(key_bytes[:].bitcast(I32), 0)
        nc.sync.dma_start(slots[:], offs)
        nc.sync.dma_start(edits[:], offs2)
        nc.sync.dma_start(q_raw[:], query.rearrange("(p t) q -> p t q", t=PACK))
        nc.sync.dma_start(eq_raw[:], equery.rearrange("(p t) q -> p t q", t=PACK))
        for quad in range(4):
            nc.scalar.dma_start(
                key_bytes[32 * quad : 32 * quad + 4, :].bitcast(I32),
                keys_scales[0, 4 * quad : 4 * quad + 4, :].bitcast(I32),
            )
        nc.sync.dma_start(key_words[:], keys_words[0].rearrange("p n t -> p (n t)").bitcast(I32))
        nc.sync.dma_start(ek_raw[0][:], ek_pairs[0])
        load_rows(ev_raw[0], evals, 0)
        nc.sync.dma_start(th_col[:], th)
        nc.sync.dma_start(ek_raw[1][:], ek_pairs[1])
        load_rows(ev_raw[1], evals, 1)
        nc.sync.dma_start(size_col[:], size.rearrange("o (p t) -> (o p) t", t=PACK))
        load_rows(ev_raw[2], evals, 2)
        nc.sync.dma_start(ew_col[:], ew.rearrange("o (p t) -> (o p) t", t=PACK))
        load_rows(ev_raw[3], evals, 3)
        for b in range(BLOCKS):
            load_rows(v_raw[b], vals, b)
        make_identity(nc, ident[:])

        def group_queries(raw, grouped):
            nc.scalar.copy(grouped[:], raw[:].rearrange("p t q -> p q t"))
            return grouped[:].rearrange("p q t -> p (q t)")

        def turn_weights(name, rows, factor, bank, of=None):
            turned = psum.tile([P, PACK, Q], F32, name=name + "_turned", tag=bank)
            for t in range(PACK):
                nc.tensor.transpose(turned[:, t, :], rows[:, t, :], ident[:])
            grouped = fresh_or_tenant(name + "_grouped", [P, Q, PACK], BF16, of, 0)
            nc.vector.tensor_tensor(
                grouped[:],
                turned[:].rearrange("p t q -> p q t"),
                factor[:].unsqueeze(1).to_broadcast([P, Q, PACK]),
                ALU.mult,
            )
            return grouped[:].rearrange("p q t -> p (q t)")

        def pick_values(name, raw, offsets, of=None, at=0):
            picked = fresh_or_tenant(name + "_picked", [P, I], BF16, of, at)
            nc.vector.tensor_copy(picked[:], raw[:].indirect(offsets[:]))
            return picked

        def turn_values(name, picked, grouped, bank):
            pairs = picked[:].bitcast(F32)
            turned = psum.tile([P, 2, P], F32, name=name + "_turned", tag=bank)
            for h in range(2):
                nc.tensor.transpose(turned[:, h, :], pairs[:, h::2], ident[:])
            nc.scalar.copy(
                grouped.bitcast(F32).rearrange("p (e h) -> p e h", h=2),
                turned[:].rearrange("p h e -> p e h"),
            )

        def cast_edit_keys(paired, raw):
            nc.scalar.activation(
                paired[:].rearrange("p (u s) -> p u s", s=2), raw[:].rearrange("p s u -> p u s"), ACT.Copy
            )

        block = P * PACK

        k_codes = kept("k_codes", [P, I], U32)
        k_scales = kept("k_scales", [P, I], U8)
        nc.vector.tensor_copy(k_scales[:], key_bytes[:].indirect(slots[:]))
        q_grouped = kept("q_grouped", [P, Q, PACK], BF16)
        q_mx = quantize("q", group_queries(q_raw, q_grouped), Q)
        eq_grouped = kept("eq_grouped", [P, Q, PACK], BF16)
        eq_mx = quantize("eq", group_queries(eq_raw, eq_grouped), Q)
        nc.vector.tensor_copy(k_codes[:], key_words[:].bitcast(U32).indirect(slots[:]))
        scores = psum.tile([P, I], F32, name="scores", tag="attn")
        product(scores[:], q_mx, (k_codes, k_scales), True, True)

        neg_max = kept("neg_max", [P, 1], F32)
        nc.vector.tensor_reduce(neg_max[:], scores[:], AX.X, ALU.max, negate=True)
        ek_paired = [kept("ek_paired%d" % h, [P, 2 * U], BF16) for h in range(2)]
        cast_edit_keys(ek_paired[0], ek_raw[0])
        p_rows = tenant("p_rows", [P, PACK, P], F32, "ek_raw0")
        row_sum = kept("row_sum", [P, 1], F32)
        nc.scalar.activation(
            p_rows[:], scores[:].rearrange("q (p t) -> q t p", t=PACK), ACT.Exp, bias=neg_max[:], accum_out=row_sum[:]
        )

        ev_picked0 = pick_values("ev0", ev_raw[0], edits)
        ek_picked = host("ek_picked", [P, 2, J], F32, 4 * KIB)
        nc.vector.tensor_copy(ek_picked[:, 0, :], ek_paired[0][:].bitcast(F32).indirect(edits[:]))
        inv_sum = kept("inv_sum", [P, 1], F32)
        nc.vector.reciprocal(inv_sum[:], row_sum[:])
        cast_edit_keys(ek_paired[1], ek_raw[1])
        p_norm = tenant("p_norm", [P, PACK, P], F32, "ek_raw1")
        nc.scalar.activation(p_norm[:], p_rows[:], ACT.Copy, scale=inv_sum[:])
        ev_grouped0 = tenant("ev_grouped0", [P, 2 * block], BF16, "ek_raw1", 2 * KIB)
        turn_values("ev0", ev_picked0, ev_grouped0[:, 0:block], "even")
        ev_picked1 = pick_values("ev1", ev_raw[1], edits)
        turn_values("ev1", ev_picked1, ev_grouped0[:, block : 2 * block], "odd")

        nc.vector.tensor_copy(ek_picked[:, 1, :], ek_paired[1][:].bitcast(F32).indirect(edits[:]))
        ek_grouped = kept("ek_grouped", [P, J * PACK], BF16)
        nc.scalar.copy(
            ek_grouped[:].bitcast(F32).rearrange("p (j h) -> p j h", h=2), ek_picked[:].rearrange("p h j -> p j h")
        )
        ev_picked2 = pick_values("ev2", ev_raw[2], edits, "ek_raw1", 4 * KIB)
        w_grouped = turn_weights("w", p_norm, size_col, "attn")
        ek_mx = quantize("ek", ek_grouped[:], J)
        e_scores = psum.tile([P, J], F32, name="e_scores", tag="edit")
        product(e_scores[:], eq_mx, ek_mx, True, True)
        neg_th = tenant("neg_th", [P, 1], F32, "ek_raw1", 5 * KIB)
        nc.scalar.mul(neg_th[:], th_col[:], -1.0)
        u_rows = kept("u_rows", [P, PACK, P], F32)
        nc.scalar.activation(
            u_rows[:], e_scores[:].rearrange("q (p t) -> q t p", t=PACK), ACT.Relu, bias=neg_th[:]
        )
        ev_grouped1 = kept("ev_grouped1", [P, 2 * block], BF16)
        turn_values("ev2", ev_picked2, ev_grouped1[:, 0:block], "attn")
        ev_picked3 = pick_values("ev3", ev_raw[3], edits, "ek_picked")
        turn_values("ev3", ev_picked3, ev_grouped1[:, block : 2 * block], "even")
        ev_mx0 = quantize("ev0", ev_grouped0[:], 2 * P)

        v_grouped01 = tenant("v_grouped01", [P, 2 * block], BF16, "neg_th")
        v_grouped2 = kept("v_grouped2", [P, block], BF16)
        v_grouped3 = kept("v_grouped3", [P, block], BF16)
        v_picked0 = pick_values("v0", v_raw[0], slots)
        v_picked1 = pick_values("v1", v_raw[1], slots)
        u_grouped = turn_weights("u", u_rows, ew_col, "edit", "v_raw1")
        turn_values("v0", v_picked0, v_grouped01[:, 0:block], "edit")
        turn_values("v1", v_picked1, v_grouped01[:, block : 2 * block], "odd")
        v_picked2 = pick_values("v2", v_raw[2], slots)
        turn_values("v2", v_picked2, v_grouped2[:], "even")
        v_picked3 = pick_values("v3", v_raw[3], slots)
        turn_values("v3", v_picked3, v_grouped3[:], "odd")
        u_mx = quantize("u", u_grouped, Q, "v_raw3")
        w_mx = quantize("w", w_grouped, Q, "v_raw3", 3 * KIB)
        ev_mx1 = quantize("ev1", ev_grouped1[:], 2 * P, "v_raw3", 4 * KIB)

        def finish(name, ev_mx, v_mx, start, count):
            acc = psum.tile([P, count], F32, name=name + "_acc")
            product(acc[:], u_mx, ev_mx, True, False)
            product(acc[:], w_mx, v_mx, False, True)
            result = kept(name + "_result", [P, count], F32)
            nc.scalar.copy(result[:], acc[:])
            nc.sync.dma_start(out[:, start : start + count], result[:])

        finish("o01", ev_mx0, quantize("v01", v_grouped01[:], 2 * P, "v_raw3", KIB), 0, 2 * P)
        finish("o2", columns(ev_mx1, 0, P), quantize("v2", v_grouped2[:], P, "v_raw3", 2 * KIB), 2 * P, P)
        finish("o3", columns(ev_mx1, P, P), quantize("v3", v_grouped3[:], P), 3 * P, P)
